import numpy as np
import ml_dtypes

BF16 = ml_dtypes.bfloat16


def bf(x):
    return np.asarray(x, np.float32).astype(BF16)


def f32(x):
    return np.asarray(x, np.float32)


def f64(x):
    return np.asarray(x).astype(np.float64)


def striped(idx):
    return np.tile(idx.reshape(-1, 16).T, (8, 1))


def rows(idx, k):
    return np.tile(idx, (k, 1))


def look(tab, idx):
    return np.take_along_axis(f64(tab), rows(idx, len(tab)), axis=1)


K, S, V, N, M = 128, 2048, 2048, 2048, 512


def setup_inputs():
    return {"tab": f32(np.random.standard_normal((2, K, S))), "w": bf(np.random.standard_normal((K, M)) / np.sqrt(K)), "b": f32(0.5 * np.random.standard_normal((M, 1))), "offs": striped(np.random.permutation(S)[:N])}


def reference(tab, w, b, offs):
    idx = offs[:16].T.reshape(-1)
    x = ((look(tab[0], idx) - 0.125) * 1.5) * (np.maximum(look(tab[1], idx), 0.0))
    return np.maximum(f64(w).T @ x + f64(b), 0.0)

@@ -1,0 +1,56 @@
+import concourse.mybir as mybir
+
+F32, BF16, U16 = mybir.dt.float32, mybir.dt.bfloat16, mybir.dt.uint16
+OP = mybir.AluOpType
+RELU = mybir.ActivationFunctionType.Relu
+
+P = 128
+N = 2048
+M = 512
+BLOCKS = M // P
+PIECE = 512
+PER_COLUMN = 16
+
+FLOPS = 2 * P * M * N
+BYTES = 4 * 2 * P * N + 2 * P * M + 4 * M + 2 * P * N // PER_COLUMN + 4 * M * N
+
+
+def tile_lookup_vg_nrmrelu_relu_kernel(tc, tab, w, b, offs, out):
+    nc = tc.nc
+    out_blocks = out.rearrange("(p t) i -> p t i", t=BLOCKS)
+    with (
+        tc.tile_pool(name="held", bufs=1) as held,
+        tc.tile_pool(name="work", bufs=4) as work,
+        tc.tile_pool(name="stage", bufs=16) as stage,
+        tc.psum_pool(name="psum", bufs=8) as psum,
+    ):
+        offsets = held.tile([P, N // PER_COLUMN], U16, name="offsets")
+        values = held.tile([P, N], F32, name="values")
+        gates = held.tile([P, N], F32, name="gates")
+        weights = held.tile([P, M], BF16, name="weights")
+        bias = held.tile([P, BLOCKS], F32, name="bias")
+        nc.sync.dma_start(offsets[:], offs)
+        nc.sync.dma_start(values[:], tab[0])
+        nc.sync.dma_start(gates[:], tab[1])
+        nc.sync.dma_start(weights[:], w)
+        nc.sync.dma_start(bias[:], b.rearrange("(p t) o -> p (t o)", t=BLOCKS))
+        block_weights = weights[:].rearrange("r (p t) -> r t p", t=BLOCKS)
+
+        for start in range(0, N, PIECE):
+            columns = slice(start, start + PIECE)
+            entries = offsets[:, start // PER_COLUMN : (start + PIECE) // PER_COLUMN]
+            value = work.tile([P, PIECE], F32, name="value")
+            nc.vector.tensor_scalar(value[:], values[:].indirect(entries), 0.125, 1.5, OP.subtract, OP.mult)
+            gate = work.tile([P, PIECE], F32, name="gate")
+            nc.scalar.activation(gate[:], gates[:].indirect(entries), RELU)
+            x = work.tile([P, PIECE], BF16, name="x")
+            nc.vector.tensor_tensor(x[:], value[:], gate[:], OP.mult)
+            for t in range(BLOCKS):
+                bank = psum.tile([P, PIECE], F32, name="bank")
+                nc.tensor.matmul(bank[:], block_weights[:, t, :], x[:], start=True, stop=True)
+                result = stage.tile([P, PIECE], F32, name="result")
+                if t % 2 == 0:
+                    nc.scalar.activation(result[:], bank[:], RELU, bias=bias[:, t : t + 1])
+                else:
+                    nc.vector.tensor_scalar(result[:], bank[:], bias[:, t : t + 1], 0.0, OP.add, OP.max)
+                nc.sync.dma_start(out_blocks[:, t, columns], result[:])

@@ -8,7 +8,8 @@ P = 128
 N = 2048
 M = 512
 BLOCKS = M // P
-PIECE = 512
+BANK = 512
+PIECES = [BANK // 2] + [BANK] * (N // BANK - 1) + [BANK // 2]
 PER_COLUMN = 16
 
 FLOPS = 2 * P * M * N
@@ -20,8 +21,10 @@ def tile_lookup_vg_nrmrelu_relu_kernel(tc, tab, w, b, offs, out):
     out_blocks = out.rearrange("(p t) i -> p t i", t=BLOCKS)
     with (
         tc.tile_pool(name="held", bufs=1) as held,
-        tc.tile_pool(name="work", bufs=4) as work,
-        tc.tile_pool(name="stage", bufs=16) as stage,
+        tc.tile_pool(name="value_ring", bufs=3) as value_ring,
+        tc.tile_pool(name="gate_ring", bufs=2) as gate_ring,
+        tc.tile_pool(name="x_ring", bufs=2) as x_ring,
+        tc.tile_pool(name="stage", bufs=20) as stage,
         tc.psum_pool(name="psum", bufs=8) as psum,
     ):
         offsets = held.tile([P, N // PER_COLUMN], U16, name="offsets")
@@ -30,27 +33,30 @@ def tile_lookup_vg_nrmrelu_relu_kernel(tc, tab, w, b, offs, out):
         weights = held.tile([P, M], BF16, name="weights")
         bias = held.tile([P, BLOCKS], F32, name="bias")
         nc.sync.dma_start(offsets[:], offs)
+        nc.sync.dma_start(weights[:], w)
         nc.sync.dma_start(values[:], tab[0])
         nc.sync.dma_start(gates[:], tab[1])
-        nc.sync.dma_start(weights[:], w)
         nc.sync.dma_start(bias[:], b.rearrange("(p t) o -> p (t o)", t=BLOCKS))
-        block_weights = weights[:].rearrange("r (p t) -> r t p", t=BLOCKS)
+        block_weights = held.tile([P, BLOCKS, P], BF16, name="block_weights")
+        nc.scalar.copy(block_weights[:], weights[:].rearrange("r (p t) -> r t p", t=BLOCKS))
 
-        for start in range(0, N, PIECE):
-            columns = slice(start, start + PIECE)
-            entries = offsets[:, start // PER_COLUMN : (start + PIECE) // PER_COLUMN]
-            value = work.tile([P, PIECE], F32, name="value")
+        start = 0
+        for width in PIECES:
+            stop = start + width
+            entries = offsets[:, start // PER_COLUMN : stop // PER_COLUMN]
+            value = value_ring.tile([P, width], F32, name="value")
             nc.vector.tensor_scalar(value[:], values[:].indirect(entries), 0.125, 1.5, OP.subtract, OP.mult)
-            gate = work.tile([P, PIECE], F32, name="gate")
+            gate = gate_ring.tile([P, width], F32, name="gate")
             nc.scalar.activation(gate[:], gates[:].indirect(entries), RELU)
-            x = work.tile([P, PIECE], BF16, name="x")
+            x = x_ring.tile([P, width], BF16, name="x")
             nc.vector.tensor_tensor(x[:], value[:], gate[:], OP.mult)
             for t in range(BLOCKS):
-                bank = psum.tile([P, PIECE], F32, name="bank")
+                bank = psum.tile([P, width], F32, name="bank")
                 nc.tensor.matmul(bank[:], block_weights[:, t, :], x[:], start=True, stop=True)
-                result = stage.tile([P, PIECE], F32, name="result")
+                result = stage.tile([P, width], F32, name="result")
                 if t % 2 == 0:
                     nc.scalar.activation(result[:], bank[:], RELU, bias=bias[:, t : t + 1])
                 else:
                     nc.vector.tensor_scalar(result[:], bank[:], bias[:, t : t + 1], 0.0, OP.add, OP.max)
-                nc.sync.dma_start(out_blocks[:, t, columns], result[:])
+                nc.sync.dma_start(out_blocks[:, t, start:stop], result[:])
+            start = stop

@@ -9,7 +9,8 @@ N = 2048
 M = 512
 BLOCKS = M // P
 BANK = 512
-PIECES = [BANK // 2] + [BANK] * (N // BANK - 1) + [BANK // 2]
+PIECES = [BANK // 4, BANK // 4, BANK // 2] + [BANK] * (N // BANK - 1)
+STORE = 2 * BANK
 PER_COLUMN = 16
 
 FLOPS = 2 * P * M * N
@@ -21,10 +22,10 @@ def tile_lookup_vg_nrmrelu_relu_kernel(tc, tab, w, b, offs, out):
     out_blocks = out.rearrange("(p t) i -> p t i", t=BLOCKS)
     with (
         tc.tile_pool(name="held", bufs=1) as held,
-        tc.tile_pool(name="value_ring", bufs=3) as value_ring,
-        tc.tile_pool(name="gate_ring", bufs=2) as gate_ring,
-        tc.tile_pool(name="x_ring", bufs=2) as x_ring,
-        tc.tile_pool(name="stage", bufs=20) as stage,
+        tc.tile_pool(name="value_ring", bufs=4) as value_ring,
+        tc.tile_pool(name="gate_ring", bufs=4) as gate_ring,
+        tc.tile_pool(name="x_ring", bufs=4) as x_ring,
+        tc.tile_pool(name="stage", bufs=12) as stage,
         tc.psum_pool(name="psum", bufs=8) as psum,
     ):
         offsets = held.tile([P, N // PER_COLUMN], U16, name="offsets")
@@ -33,30 +34,49 @@ def tile_lookup_vg_nrmrelu_relu_kernel(tc, tab, w, b, offs, out):
         weights = held.tile([P, M], BF16, name="weights")
         bias = held.tile([P, BLOCKS], F32, name="bias")
         nc.sync.dma_start(offsets[:], offs)
-        nc.sync.dma_start(weights[:], w)
+        nc.sync.dma_start(bias[:], b.rearrange("(p t) o -> p (t o)", t=BLOCKS))
         nc.sync.dma_start(values[:], tab[0])
         nc.sync.dma_start(gates[:], tab[1])
-        nc.sync.dma_start(bias[:], b.rearrange("(p t) o -> p (t o)", t=BLOCKS))
-        block_weights = held.tile([P, BLOCKS, P], BF16, name="block_weights")
-        nc.scalar.copy(block_weights[:], weights[:].rearrange("r (p t) -> r t p", t=BLOCKS))
+        nc.sync.dma_start(weights[:], w)
+        block_weights = weights[:].rearrange("r (p t) -> r t p", t=BLOCKS)
 
-        start = 0
-        for width in PIECES:
-            stop = start + width
-            entries = offsets[:, start // PER_COLUMN : stop // PER_COLUMN]
+        warm = held.tile([P, 1], F32, name="warm")
+        nc.vector.memset(warm[:], 0.0)
+        warmed = held.tile([P, 1], F32, name="warmed")
+        nc.scalar.activation(warmed[:], warm[:], RELU)
+
+
+        def look_up(start, width):
+            entries = offsets[:, start // PER_COLUMN : (start + width) // PER_COLUMN]
             value = value_ring.tile([P, width], F32, name="value")
             nc.vector.tensor_scalar(value[:], values[:].indirect(entries), 0.125, 1.5, OP.subtract, OP.mult)
             gate = gate_ring.tile([P, width], F32, name="gate")
             nc.scalar.activation(gate[:], gates[:].indirect(entries), RELU)
             x = x_ring.tile([P, width], BF16, name="x")
             nc.vector.tensor_tensor(x[:], value[:], gate[:], OP.mult)
-            for t in range(BLOCKS):
-                bank = psum.tile([P, width], F32, name="bank")
-                nc.tensor.matmul(bank[:], block_weights[:, t, :], x[:], start=True, stop=True)
-                result = stage.tile([P, width], F32, name="result")
-                if t % 2 == 0:
-                    nc.scalar.activation(result[:], bank[:], RELU, bias=bias[:, t : t + 1])
-                else:
-                    nc.vector.tensor_scalar(result[:], bank[:], bias[:, t : t + 1], 0.0, OP.add, OP.max)
-                nc.sync.dma_start(out_blocks[:, t, start:stop], result[:])
-            start = stop
+            return x
+
+        def dense(x, start, width):
+            group = min(BLOCKS, STORE // width)
+            for first in range(0, BLOCKS, group):
+                results = stage.tile([P, group, width], F32, name="results")
+                for t in range(first, first + group):
+                    bank = psum.tile([P, width], F32, name="bank")
+                    nc.tensor.matmul(bank[:], block_weights[:, t, :], x[:], start=True, stop=True)
+                    if t % 2 == 0:
+                        nc.scalar.activation(results[:, t - first, :], bank[:], RELU, bias=bias[:, t : t + 1])
+                    else:
+                        nc.vector.tensor_scalar(
+                            results[:, t - first, :], bank[:], bias[:, t : t + 1], 0.0, OP.add, OP.max
+                        )
+                nc.sync.dma_start(out_blocks[:, first : first + group, start : start + width], results[:])
+
+        start = 0
+        waiting = None
+        for width in PIECES:
+            x = look_up(start, width)
+            if waiting is not None:
+                dense(*waiting)
+            waiting = (x, start, width)
+            start += width
+        dense(*waiting)

@@ -53,7 +53,8 @@ def tile_lookup_vg_nrmrelu_relu_kernel(tc, tab, w, b, offs, out):
             gate = gate_ring.tile([P, width], F32, name="gate")
             nc.scalar.activation(gate[:], gates[:].indirect(entries), RELU)
             x = x_ring.tile([P, width], BF16, name="x")
-            nc.vector.tensor_tensor(x[:], value[:], gate[:], OP.mult)
+            multiplier = nc.gpsimd if width == BANK else nc.vector
+            multiplier.tensor_tensor(x[:], value[:], gate[:], OP.mult)
             return x
 
         def dense(x, start, width):

import concourse.mybir as mybir

F32, BF16, U16 = mybir.dt.float32, mybir.dt.bfloat16, mybir.dt.uint16
OP = mybir.AluOpType
RELU = mybir.ActivationFunctionType.Relu

P = 128
N = 2048
M = 512
BLOCKS = M // P
BANK = 512
PIECES = [BANK // 4, BANK // 4, BANK // 2] + [BANK] * (N // BANK - 1)
STORE = 2 * BANK
PER_COLUMN = 16

FLOPS = 2 * P * M * N
BYTES = 4 * 2 * P * N + 2 * P * M + 4 * M + 2 * P * N // PER_COLUMN + 4 * M * N


def tile_lookup_vg_nrmrelu_relu_kernel(tc, tab, w, b, offs, out):
    nc = tc.nc
    out_blocks = out.rearrange("(p t) i -> p t i", t=BLOCKS)
    with (
        tc.tile_pool(name="held", bufs=1) as held,
        tc.tile_pool(name="value_ring", bufs=4) as value_ring,
        tc.tile_pool(name="gate_ring", bufs=4) as gate_ring,
        tc.tile_pool(name="x_ring", bufs=4) as x_ring,
        tc.tile_pool(name="stage", bufs=12) as stage,
        tc.psum_pool(name="psum", bufs=8) as psum,
    ):
        offsets = held.tile([P, N // PER_COLUMN], U16, name="offsets")
        values = held.tile([P, N], F32, name="values")
        gates = held.tile([P, N], F32, name="gates")
        weights = held.tile([P, M], BF16, name="weights")
        bias = held.tile([P, BLOCKS], F32, name="bias")
        nc.sync.dma_start(offsets[:], offs)
        nc.sync.dma_start(bias[:], b.rearrange("(p t) o -> p (t o)", t=BLOCKS))
        nc.sync.dma_start(values[:], tab[0])
        nc.sync.dma_start(gates[:], tab[1])
        nc.sync.dma_start(weights[:], w)
        block_weights = weights[:].rearrange("r (p t) -> r t p", t=BLOCKS)

        warm = held.tile([P, 1], F32, name="warm")
        nc.vector.memset(warm[:], 0.0)
        warmed = held.tile([P, 1], F32, name="warmed")
        nc.scalar.activation(warmed[:], warm[:], RELU)


        def look_up(start, width):
            entries = offsets[:, start // PER_COLUMN : (start + width) // PER_COLUMN]
            value = value_ring.tile([P, width], F32, name="value")
            nc.vector.tensor_scalar(value[:], values[:].indirect(entries), 0.125, 1.5, OP.subtract, OP.mult)
            gate = gate_ring.tile([P, width], F32, name="gate")
            nc.scalar.activation(gate[:], gates[:].indirect(entries), RELU)
            x = x_ring.tile([P, width], BF16, name="x")
            multiplier = nc.gpsimd if width == BANK else nc.vector
            multiplier.tensor_tensor(x[:], value[:], gate[:], OP.mult)
            return x

        def dense(x, start, width):
            group = min(BLOCKS, STORE // width)
            for first in range(0, BLOCKS, group):
                results = stage.tile([P, group, width], F32, name="results")
                for t in range(first, first + group):
                    bank = psum.tile([P, width], F32, name="bank")
                    nc.tensor.matmul(bank[:], block_weights[:, t, :], x[:], start=True, stop=True)
                    if t % 2 == 0:
                        nc.scalar.activation(results[:, t - first, :], bank[:], RELU, bias=bias[:, t : t + 1])
                    else:
                        nc.vector.tensor_scalar(
                            results[:, t - first, :], bank[:], bias[:, t : t + 1], 0.0, OP.add, OP.max
                        )
                nc.sync.dma_start(out_blocks[:, first : first + group, start : start + width], results[:])

        start = 0
        waiting = None
        for width in PIECES:
            x = look_up(start, width)
            if waiting is not None:
                dense(*waiting)
            waiting = (x, start, width)
            start += width
        dense(*waiting)
